import numpy as np
import ml_dtypes


def mxq(x, axis, fmt="e4m3"):
    dtype, down = {"e4m3": (ml_dtypes.float8_e4m3fn, 7), "e5m2": (ml_dtypes.float8_e5m2, 14)}[fmt]
    v = np.moveaxis(np.asarray(x, np.float32).astype(ml_dtypes.bfloat16).astype(np.float64), axis, -1)
    blocks = v.reshape(v.shape[:-1] + (-1, 32))
    amax = np.abs(blocks).max(-1, keepdims=True)
    byte = np.maximum(np.where(amax > 0, np.frexp(amax)[1] - 1 + 127, 0) - down, 1)
    scale = np.exp2(byte - 127.0)
    codes = (blocks / scale).astype(np.float32).astype(dtype).astype(np.float64)
    return np.moveaxis((codes * scale).reshape(v.shape), -1, axis)


WIDE = False


def mx_kscale(k):
    if not WIDE:
        return np.ones(k)
    levels = np.array([10, -10, 5, -5, 0])
    if k % 512:
        return np.exp2(np.random.permutation(np.resize(levels, k // 32))).repeat(32)
    a = np.empty((k // 512, 16))
    for p in range(k // 512):
        a[p, :8] = np.random.permutation(np.resize(levels, 8))
        for g in range(8):
            far = levels[np.abs(levels - a[p, g]) >= 10]
            a[p, g + 8] = far[np.random.randint(len(far))]
    return np.exp2(a.ravel()).repeat(32)


BF16 = ml_dtypes.bfloat16


def bf(x):
    return np.asarray(x, np.float32).astype(BF16)


def f64(x):
    return np.asarray(x).astype(np.float64)

E4M3FN = np.array([(-1.0 if i & 128 else 1.0) * ((1.0 + (i & 7) / 8.0) * 2.0 ** (((i >> 3) & 15) - 7) if i & 120 else (i & 7) * 2.0 ** -9) for i in range(256)])


def e4m3fn_bytes(y):
    return np.clip(np.asarray(y, np.float64), -448.0, 448.0).astype(np.float32).astype(ml_dtypes.float8_e4m3fn).view(np.uint8)


def e4m3fn_values(b):
    return E4M3FN[b]


T, U, K, N, B = 512, 1024, 2048, 1536, 128
FP8_MAX = 448.0


def setup_inputs():
    s = mx_kscale(K)
    x = np.random.standard_normal((U, K)) * s
    w = np.random.standard_normal((N, K)) / np.sqrt(K) / s
    x_scale = (np.abs(x).reshape(U, K // B, B).max(axis=2) / FP8_MAX).astype(np.float32)
    w_scale = (np.abs(w).reshape(N // B, B, K // B, B).max(axis=(1, 3)) / FP8_MAX).astype(np.float32)
    x_bytes = e4m3fn_bytes(x / np.repeat(f64(x_scale), B, axis=1))
    w_bytes = e4m3fn_bytes(w / np.repeat(np.repeat(f64(w_scale), B, axis=0), B, axis=1))
    return {"h": bf(np.random.standard_normal((T, K)) * s),
            "x_bytes": x_bytes,
            "x_scale": x_scale,
            "w_bytes": w_bytes,
            "w_scale": w_scale,
            "b": bf(0.4 * np.random.standard_normal(N))}


def reference(h, x_bytes, x_scale, w_bytes, w_scale, b):
    x = e4m3fn_values(x_bytes) * np.repeat(f64(x_scale), B, axis=1)
    w = e4m3fn_values(w_bytes) * np.repeat(np.repeat(f64(w_scale), B, axis=0), B, axis=1)
    wq = mxq(w, 1, "e4m3")
    q_local = (mxq(f64(h), 1, "e4m3") @ wq.T) + f64(b)
    q_gathered = (mxq(x, 1, "e4m3") @ wq.T) + f64(b)
    return q_local, q_gathered

@@ -1,0 +1,233 @@
+from contextlib import ExitStack
+
+import concourse.mybir as mybir
+from concourse.masks import make_identity
+
+T, U, K, N, B = 512, 1024, 2048, 1536, 128
+FLOPS = 2 * (T + U) * K * N
+BYTES = T * K * 2 + U * K + N * K + U * (K // B) * 4 + (N // B) * (K // B) * 4 + N * 2 + (T + U) * N * 4
+
+F32 = mybir.dt.float32
+BF16 = mybir.dt.bfloat16
+U32 = mybir.dt.uint32
+U8 = mybir.dt.uint8
+FP8 = mybir.dt.float8_e4m3fn
+FP8X4 = mybir.dt.float8_e4m3fn_x4
+MULT = mybir.AluOpType.mult
+ADD = mybir.AluOpType.add
+COPY = mybir.ActivationFunctionType.Copy
+
+P = 128
+PASSES = K // 512
+
+UNITS = ["w0a","w0b","h0","x0","h1","w1a","w1b","x1","x2","w2a","w2b","x3"]
+LOADS = ["w0a","w0b","h0","x0","h1","w1a","w1b","x1","x2","w2a","w2b","x3"]
+SCALAR = ["w0a","w1b","x1"]
+SHUF = ["h0","h1"]
+CAPS = [4,4,4,4,4,4,4,4,4,4,4,4]
+LAG = 1
+
+
+def tile_fp8_query_projection_d2_kernel(tc, h, x_bytes, x_scale, w_bytes, w_scale, b, out_0, out_1):
+    nc = tc.nc
+    with ExitStack() as ctx:
+        const = ctx.enter_context(tc.tile_pool(name="const", bufs=1))
+        raws = ctx.enter_context(tc.tile_pool(name="raws", bufs=1))
+        wides = ctx.enter_context(tc.tile_pool(name="wides", bufs=6))
+        groups = ctx.enter_context(tc.tile_pool(name="groups", bufs=3))
+        outs = ctx.enter_context(tc.tile_pool(name="outs", bufs=6))
+        tpsum = ctx.enter_context(tc.psum_pool(name="tpsum", bufs=1))
+        mpsum = ctx.enter_context(tc.psum_pool(name="mpsum", bufs=4))
+
+        ident = const.tile([P, P], F32, name="ident", align_bytes=64)
+        make_identity(nc, ident[:])
+        ws = const.tile([P, (N // B) * (K // B)], F32, name="ws", align_bytes=64)
+        xs = const.tile([P, U // P, K // B], F32, name="xs", align_bytes=64)
+        bias = const.tile([P, N], BF16, name="bias", align_bytes=64)
+
+        raw = {}
+        wide = {}
+        bank = {}
+        grouped = {}
+        codes = {}
+        scales = {}
+        for n in range(3):
+            codes["w%d" % n] = const.tile([P, PASSES, 512], U32, name="wc%d" % n, align_bytes=64)
+            scales["w%d" % n] = const.tile([P, PASSES, 512], U8, name="wsc%d" % n, align_bytes=64)
+        for u in UNITS:
+            if u[0] != "w":
+                codes[u] = const.tile([P, PASSES, 256], U32, name="c_" + u, align_bytes=64)
+                scales[u] = const.tile([P, PASSES, 256], U8, name="s_" + u, align_bytes=64)
+
+        def row_pair(u):
+            if u[0] == "w":
+                return 2 * int(u[1]) + (1 if u[2] == "b" else 0)
+            return int(u[1])
+
+        def load(u):
+            rp = row_pair(u)
+            if u[0] == "h":
+                raw[u] = raws.tile([P, 2, K], BF16, name="raw_" + u, align_bytes=64)
+                src = h
+            else:
+                raw[u] = raws.tile([P, 2, K], U8, name="raw_" + u, align_bytes=64)
+                src = x_bytes if u[0] == "x" else w_bytes
+            nc.sync.dma_start(out=raw[u][:], in_=src[256 * rp : 256 * rp + 256, :].rearrange("(i p) k -> p i k", p=P))
+
+        def contiguous(u, i):
+            return (u[0] != "h" and not (u in SCALAR and i == 0)) or u in SHUF
+
+        def widen(u):
+            if u[0] == "h":
+                if u in SHUF:
+                    for i in range(2):
+                        wd = wides.tile([P, PASSES, 512], BF16, name="wd%d" % i, align_bytes=64)
+                        wide[u, i] = wd
+                    for g in range(PASSES):
+                        for i in range(2):
+                            nc.scalar.copy(
+                                out=wide[u, i][:, g, :].bitcast(F32).rearrange("p (u w) -> p u w", u=2),
+                                in_=raw[u][:, i, 512 * g : 512 * g + 512].bitcast(F32).rearrange("p (w u) -> p u w", u=2),
+                            )
+                return
+            rp = row_pair(u)
+            for i in range(2):
+                wd = wides.tile([P, PASSES, 512], BF16, name="wd%d" % i, align_bytes=64)
+                wide[u, i] = wd
+            for g in range(PASSES):
+                for q in range(4):
+                    for i in range(2):
+                        j = 4 * g + q
+                        m = 2 * rp + i
+                        sc = ws[:, 16 * m + j : 16 * m + j + 1] if u[0] == "w" else xs[:, m, j : j + 1]
+                        src = raw[u][:, i, 128 * j : 128 * j + 128].bitcast(FP8)
+                        if u in SCALAR and i == 0:
+                            nc.scalar.activation(out=wide[u, i][:, g, 128 * q : 128 * q + 128], in_=src, func=COPY, scale=sc)
+                        else:
+                            nc.vector.tensor_scalar(
+                                out=wide[u, i][:, g, :].rearrange("p (u w e) -> p w u e", u=2, e=2)[:, 32 * q : 32 * q + 32],
+                                in0=src.rearrange("p (w u e) -> p w u e", u=2, e=2),
+                                scalar1=sc,
+                                scalar2=None,
+                                op0=MULT,
+                            )
+
+        def transposes(u):
+            for g in range(PASSES):
+                bk = tpsum.tile([P, 2, 2, P], F32, name="t%d" % g)
+                bank[u, g] = bk
+                for i in range(2):
+                    if u[0] == "h" and u not in SHUF:
+                        words = raw[u][:, i, 512 * g : 512 * g + 512].bitcast(F32)
+                    else:
+                        words = wide[u, i][:, g, :].bitcast(F32)
+                    for t in range(2):
+                        src = words[:, P * t : P * t + P] if contiguous(u, i) else words[:, t : 256 : 2]
+                        nc.tensor.transpose(bk[:, i, t, :], src, ident[:])
+
+        def evacuate(u):
+            gr = groups.tile([P, PASSES, 1024], BF16, name="gr", align_bytes=64)
+            grouped[u] = gr
+            for g in range(PASSES):
+                nc.scalar.copy(
+                    out=gr[:, g, :].bitcast(F32).rearrange("p (i r u) -> p i r u", i=2, u=2),
+                    in_=bank[u, g][:].rearrange("p i u r -> p i r u"),
+                )
+
+        def quantize(u):
+            gr = grouped[u]
+            if u[0] == "w":
+                lo = 256 if u[2] == "b" else 0
+                key = u[:2]
+                for g in range(PASSES):
+                    nc.vector.quantize_mx(
+                        out=codes[key][:, g, lo : lo + 256].bitcast(FP8X4),
+                        scales=scales[key][:, g, lo : lo + 256],
+                        in_=gr[:, g, :],
+                    )
+            else:
+                for g in range(0, PASSES, 2):
+                    nc.vector.quantize_mx(
+                        out=codes[u][:, g : g + 2, :].rearrange("p g c -> p (g c)").bitcast(FP8X4),
+                        scales=scales[u][:, g : g + 2, :].rearrange("p g c -> p (g c)"),
+                        in_=gr[:, g : g + 2, :].rearrange("p g c -> p (g c)"),
+                    )
+
+        acc = {}
+
+        def multiply(grp):
+            u, i, n = grp
+            ps = mpsum.tile([P, 512], F32, name="acc")
+            acc[grp] = ps
+            key = "w%d" % n
+            for g in range(PASSES):
+                nc.tensor.matmul_mx(
+                    out=ps[:],
+                    lhsT=codes[u][:, g, P * i : P * i + P].bitcast(FP8X4),
+                    lhsT_scale=scales[u][:, g, P * i : P * i + P],
+                    rhs=codes[key][:, g, :].bitcast(FP8X4),
+                    rhs_scale=scales[key][:, g, :],
+                    start=(g == 0),
+                    stop=(g == PASSES - 1),
+                )
+
+        def finish(grp):
+            u, i, n = grp
+            o = outs.tile([P, 512], F32, name="o", align_bytes=64)
+            nc.vector.tensor_tensor(out=o[:], in0=acc[grp][:], in1=bias[:, 512 * n : 512 * n + 512], op=ADD)
+            dst = out_0 if u[0] == "h" else out_1
+            r0 = 256 * row_pair(u) + P * i
+            nc.sync.dma_start(out=dst[r0 : r0 + P, 512 * n : 512 * n + 512], in_=o[:])
+
+        def available(r):
+            us = UNITS[: r + 1]
+            res = []
+            for u in us:
+                if u[0] != "w":
+                    for n in range(3):
+                        if "w%da" % n in us and "w%db" % n in us:
+                            for i in range(2):
+                                res.append((u, i, n))
+            return res
+
+        with ExitStack() as sched:
+            sched.enter_context(tc.manual_schedule())
+            nc.sync.dma_start(out=ws[:], in_=w_scale.rearrange("i j -> (i j)").partition_broadcast(P))
+            for k, u in enumerate(LOADS):
+                load(u)
+                if k == 1:
+                    nc.sync.dma_start(out=xs[:], in_=x_scale.rearrange("(i p) j -> p i j", p=P))
+                if k == 5:
+                    nc.sync.dma_start(out=bias[:], in_=b.partition_broadcast(P))
+
+            R = len(UNITS)
+            done = []
+            closed = 0
+            widen(UNITS[0])
+            widen(UNITS[1])
+            transposes(UNITS[0])
+            r = 0
+            while len(done) < 36:
+                if r < R:
+                    evacuate(UNITS[r])
+                    if r + 2 < R:
+                        widen(UNITS[r + 2])
+                    if r + 1 < R:
+                        transposes(UNITS[r + 1])
+                    quantize(UNITS[r])
+                fresh = [x for x in available(min(r - LAG, R - 1)) if x not in done]
+                if r < R:
+                    fresh = fresh[: CAPS[r]]
+                for x in fresh:
+                    multiply(x)
+                    done.append(x)
+                    if r >= R and len(done) - closed > 3:
+                        finish(done[closed])
+                        closed += 1
+                while r < R and closed < len(done):
+                    finish(done[closed])
+                    closed += 1
+                r += 1
+            while closed < len(done):
+                finish(done[closed])
+                closed += 1

@@ -22,8 +22,8 @@ PASSES = K // 512
 
 UNITS = ["w0a","w0b","h0","x0","h1","w1a","w1b","x1","x2","w2a","w2b","x3"]
 LOADS = ["w0a","w0b","h0","x0","h1","w1a","w1b","x1","x2","w2a","w2b","x3"]
-SCALAR = ["w0a","w1b","x1"]
-SHUF = ["h0","h1"]
+SCALAR = ["w0a","w1b","x1","w2a","w2b","x3"]
+SHUF = []
 CAPS = [4,4,4,4,4,4,4,4,4,4,4,4]
 LAG = 1
 
@@ -75,7 +75,7 @@ def tile_fp8_query_projection_d2_kernel(tc, h, x_bytes, x_scale, w_bytes, w_scal
             nc.sync.dma_start(out=raw[u][:], in_=src[256 * rp : 256 * rp + 256, :].rearrange("(i p) k -> p i k", p=P))
 
         def contiguous(u, i):
-            return (u[0] != "h" and not (u in SCALAR and i == 0)) or u in SHUF
+            return u in SHUF
 
         def widen(u):
             if u[0] == "h":
@@ -105,8 +105,8 @@ def tile_fp8_query_projection_d2_kernel(tc, h, x_bytes, x_scale, w_bytes, w_scal
                             nc.scalar.activation(out=wide[u, i][:, g, 128 * q : 128 * q + 128], in_=src, func=COPY, scale=sc)
                         else:
                             nc.vector.tensor_scalar(
-                                out=wide[u, i][:, g, :].rearrange("p (u w e) -> p w u e", u=2, e=2)[:, 32 * q : 32 * q + 32],
-                                in0=src.rearrange("p (w u e) -> p w u e", u=2, e=2),
+                                out=wide[u, i][:, g, 128 * q : 128 * q + 128],
+                                in0=src,
                                 scalar1=sc,
                                 scalar2=None,
                                 op0=MULT,

@@ -20,12 +20,12 @@ COPY = mybir.ActivationFunctionType.Copy
 P = 128
 PASSES = K // 512
 
-UNITS = ["w0a","w0b","h0","x0","h1","w1a","w1b","x1","x2","w2a","w2b","x3"]
-LOADS = ["w0a","w0b","h0","x0","h1","w1a","w1b","x1","x2","w2a","w2b","x3"]
-SCALAR = ["w0a","w1b","x1","w2a","w2b","x3"]
+UNITS = ["w0a","h0","w0b","h1","w1a","w1b","x0","x1","x2","w2a","w2b","x3"]
+LOADS = ["w0a","h0","w0b","h1","w1a","w1b","x0","x1","x2","w2a","w2b","x3"]
+SCALAR = ["w0a","w0b","w1a","w1b","x0","x1","x2","w2a","w2b","x3"]
 SHUF = []
-CAPS = [4,4,4,4,4,4,4,4,4,4,4,4]
-LAG = 1
+CAP = 3
+SHARED = ["w0a","h0","w0b","h1"]
 
 
 def tile_fp8_query_projection_d2_kernel(tc, h, x_bytes, x_scale, w_bytes, w_scale, b, out_0, out_1):
@@ -72,10 +72,13 @@ def tile_fp8_query_projection_d2_kernel(tc, h, x_bytes, x_scale, w_bytes, w_scal
             else:
                 raw[u] = raws.tile([P, 2, K], U8, name="raw_" + u, align_bytes=64)
                 src = x_bytes if u[0] == "x" else w_bytes
-            nc.sync.dma_start(out=raw[u][:], in_=src[256 * rp : 256 * rp + 256, :].rearrange("(i p) k -> p i k", p=P))
+            cuts = 2 if u == LOADS[0] else 1
+            for c in range(cuts):
+                cols = slice(c * K // cuts, (c + 1) * K // cuts)
+                nc.sync.dma_start(out=raw[u][:, :, cols], in_=src[256 * rp : 256 * rp + 256, cols].rearrange("(i p) k -> p i k", p=P))
 
         def contiguous(u, i):
-            return u in SHUF
+            return (u[0] != "h" and not (u in SCALAR and i == 0)) or u in SHUF
 
         def widen(u):
             if u[0] == "h":
@@ -105,8 +108,8 @@ def tile_fp8_query_projection_d2_kernel(tc, h, x_bytes, x_scale, w_bytes, w_scal
                             nc.scalar.activation(out=wide[u, i][:, g, 128 * q : 128 * q + 128], in_=src, func=COPY, scale=sc)
                         else:
                             nc.vector.tensor_scalar(
-                                out=wide[u, i][:, g, 128 * q : 128 * q + 128],
-                                in0=src,
+                                out=wide[u, i][:, g, :].rearrange("p (u w e) -> p w u e", u=2, e=2)[:, 32 * q : 32 * q + 32],
+                                in0=src.rearrange("p (w u e) -> p w u e", u=2, e=2),
                                 scalar1=sc,
                                 scalar2=None,
                                 op0=MULT,
@@ -129,7 +132,8 @@ def tile_fp8_query_projection_d2_kernel(tc, h, x_bytes, x_scale, w_bytes, w_scal
             gr = groups.tile([P, PASSES, 1024], BF16, name="gr", align_bytes=64)
             grouped[u] = gr
             for g in range(PASSES):
-                nc.scalar.copy(
+                copy = nc.vector.tensor_copy if u in SHARED and g == PASSES - 1 else nc.scalar.copy
+                copy(
                     out=gr[:, g, :].bitcast(F32).rearrange("p (i r u) -> p i r u", i=2, u=2),
                     in_=bank[u, g][:].rearrange("p i u r -> p i r u"),
                 )
@@ -156,38 +160,47 @@ def tile_fp8_query_projection_d2_kernel(tc, h, x_bytes, x_scale, w_bytes, w_scal
         acc = {}
 
         def multiply(grp):
-            u, i, n = grp
+            u, i, n, lo, hi = grp
             ps = mpsum.tile([P, 512], F32, name="acc")
             acc[grp] = ps
             key = "w%d" % n
             for g in range(PASSES):
                 nc.tensor.matmul_mx(
-                    out=ps[:],
+                    out=ps[:, 0 : hi - lo],
                     lhsT=codes[u][:, g, P * i : P * i + P].bitcast(FP8X4),
                     lhsT_scale=scales[u][:, g, P * i : P * i + P],
-                    rhs=codes[key][:, g, :].bitcast(FP8X4),
-                    rhs_scale=scales[key][:, g, :],
+                    rhs=codes[key][:, g, lo:hi].bitcast(FP8X4),
+                    rhs_scale=scales[key][:, g, lo:hi],
                     start=(g == 0),
                     stop=(g == PASSES - 1),
                 )
 
         def finish(grp):
-            u, i, n = grp
+            u, i, n, lo, hi = grp
             o = outs.tile([P, 512], F32, name="o", align_bytes=64)
-            nc.vector.tensor_tensor(out=o[:], in0=acc[grp][:], in1=bias[:, 512 * n : 512 * n + 512], op=ADD)
+            c0 = 512 * n + lo
+            c1 = 512 * n + hi
+            nc.vector.tensor_tensor(out=o[:, 0 : hi - lo], in0=acc[grp][:, 0 : hi - lo], in1=bias[:, c0:c1], op=ADD)
             dst = out_0 if u[0] == "h" else out_1
             r0 = 256 * row_pair(u) + P * i
-            nc.sync.dma_start(out=dst[r0 : r0 + P, 512 * n : 512 * n + 512], in_=o[:])
+            nc.sync.dma_start(out=dst[r0 : r0 + P, c0:c1], in_=o[:, 0 : hi - lo])
 
-        def available(r):
+        def available(r, done):
             us = UNITS[: r + 1]
             res = []
-            for u in us:
-                if u[0] != "w":
-                    for n in range(3):
-                        if "w%da" % n in us and "w%db" % n in us:
-                            for i in range(2):
-                                res.append((u, i, n))
+            for n in range(3):
+                ready = [("w%d%s" % (n, c)) in us for c in "ab"]
+                for u in us:
+                    if u[0] == "w":
+                        continue
+                    for i in range(2):
+                        left = [ready[k] and (u, i, n, k) not in done for k in range(2)]
+                        if left[0] and left[1]:
+                            res.append((u, i, n, 0, 512))
+                        elif True:
+                            for k in range(2):
+                                if left[k]:
+                                    res.append((u, i, n, 256 * k, 256 * k + 256))
             return res
 
         with ExitStack() as sched:
@@ -201,13 +214,14 @@ def tile_fp8_query_projection_d2_kernel(tc, h, x_bytes, x_scale, w_bytes, w_scal
                     nc.sync.dma_start(out=bias[:], in_=b.partition_broadcast(P))
 
             R = len(UNITS)
-            done = []
+            done = set()
+            order = []
             closed = 0
             widen(UNITS[0])
             widen(UNITS[1])
             transposes(UNITS[0])
             r = 0
-            while len(done) < 36:
+            while len(done) < 72:
                 if r < R:
                     evacuate(UNITS[r])
                     if r + 2 < R:
@@ -215,19 +229,23 @@ def tile_fp8_query_projection_d2_kernel(tc, h, x_bytes, x_scale, w_bytes, w_scal
                     if r + 1 < R:
                         transposes(UNITS[r + 1])
                     quantize(UNITS[r])
-                fresh = [x for x in available(min(r - LAG, R - 1)) if x not in done]
-                if r < R:
-                    fresh = fresh[: CAPS[r]]
-                for x in fresh:
+                room = 512 * CAP if r < R else 512 * 36
+                for x in available(min(r - 1, R - 1), done):
+                    u, i, n, lo, hi = x
+                    if hi - lo > room:
+                        break
+                    room -= hi - lo
                     multiply(x)
-                    done.append(x)
-                    if r >= R and len(done) - closed > 3:
-                        finish(done[closed])
+                    order.append(x)
+                    for k in range(lo // 256, hi // 256):
+                        done.add((u, i, n, k))
+                    if r >= R and len(order) - closed > 3:
+                        finish(order[closed])
                         closed += 1
-                while r < R and closed < len(done):
-                    finish(done[closed])
+                while r < R and closed < len(order):
+                    finish(order[closed])
                     closed += 1
                 r += 1
-            while closed < len(done):
-                finish(done[closed])
+            while closed < len(order):
+                finish(order[closed])
                 closed += 1

@@ -22,10 +22,11 @@ PASSES = K // 512
 
 UNITS = ["w0a","h0","w0b","h1","w1a","w1b","x0","x1","x2","w2a","w2b","x3"]
 LOADS = ["w0a","h0","w0b","h1","w1a","w1b","x0","x1","x2","w2a","w2b","x3"]
-SCALAR = ["w0a","w0b","w1a","w1b","x0","x1","x2","w2a","w2b","x3"]
+SCALAR = ["w0a","w1b","x0","x1","x2","w2a","w2b","x3"]
 SHUF = []
+RUN = 2
 CAP = 3
-SHARED = ["w0a","h0","w0b","h1"]
+SHARED = []
 
 
 def tile_fp8_query_projection_d2_kernel(tc, h, x_bytes, x_scale, w_bytes, w_scale, b, out_0, out_1):
@@ -64,6 +65,9 @@ def tile_fp8_query_projection_d2_kernel(tc, h, x_bytes, x_scale, w_bytes, w_scal
                 return 2 * int(u[1]) + (1 if u[2] == "b" else 0)
             return int(u[1])
 
+        def row_tiles(t, u):
+            return t.rearrange("(p i) k -> p i k", p=P) if u[0] == "x" else t.rearrange("(i p) k -> p i k", p=P)
+
         def load(u):
             rp = row_pair(u)
             if u[0] == "h":
@@ -75,7 +79,7 @@ def tile_fp8_query_projection_d2_kernel(tc, h, x_bytes, x_scale, w_bytes, w_scal
             cuts = 2 if u == LOADS[0] else 1
             for c in range(cuts):
                 cols = slice(c * K // cuts, (c + 1) * K // cuts)
-                nc.sync.dma_start(out=raw[u][:, :, cols], in_=src[256 * rp : 256 * rp + 256, cols].rearrange("(i p) k -> p i k", p=P))
+                nc.sync.dma_start(out=raw[u][:, :, cols], in_=row_tiles(src, u)[:, 2 * rp : 2 * rp + 2, cols])
 
         def contiguous(u, i):
             return (u[0] != "h" and not (u in SCALAR and i == 0)) or u in SHUF
@@ -115,8 +119,8 @@ def tile_fp8_query_projection_d2_kernel(tc, h, x_bytes, x_scale, w_bytes, w_scal
                                 op0=MULT,
                             )
 
-        def transposes(u):
-            for g in range(PASSES):
+        def transposes(u, passes):
+            for g in passes:
                 bk = tpsum.tile([P, 2, 2, P], F32, name="t%d" % g)
                 bank[u, g] = bk
                 for i in range(2):
@@ -182,8 +186,7 @@ def tile_fp8_query_projection_d2_kernel(tc, h, x_bytes, x_scale, w_bytes, w_scal
             c1 = 512 * n + hi
             nc.vector.tensor_tensor(out=o[:, 0 : hi - lo], in0=acc[grp][:, 0 : hi - lo], in1=bias[:, c0:c1], op=ADD)
             dst = out_0 if u[0] == "h" else out_1
-            r0 = 256 * row_pair(u) + P * i
-            nc.sync.dma_start(out=dst[r0 : r0 + P, c0:c1], in_=o[:, 0 : hi - lo])
+            nc.sync.dma_start(out=row_tiles(dst, u)[:, 2 * row_pair(u) + i, c0:c1], in_=o[:, 0 : hi - lo])
 
         def available(r, done):
             us = UNITS[: r + 1]
@@ -209,7 +212,7 @@ def tile_fp8_query_projection_d2_kernel(tc, h, x_bytes, x_scale, w_bytes, w_scal
             for k, u in enumerate(LOADS):
                 load(u)
                 if k == 1:
-                    nc.sync.dma_start(out=xs[:], in_=x_scale.rearrange("(i p) j -> p i j", p=P))
+                    nc.sync.dma_start(out=xs[:], in_=x_scale.rearrange("(p i) j -> p i j", p=P))
                 if k == 5:
                     nc.sync.dma_start(out=bias[:], in_=b.partition_broadcast(P))
 
@@ -219,22 +222,23 @@ def tile_fp8_query_projection_d2_kernel(tc, h, x_bytes, x_scale, w_bytes, w_scal
             closed = 0
             widen(UNITS[0])
             widen(UNITS[1])
-            transposes(UNITS[0])
+            transposes(UNITS[0], range(PASSES))
             r = 0
             while len(done) < 72:
                 if r < R:
                     evacuate(UNITS[r])
                     if r + 2 < R:
                         widen(UNITS[r + 2])
-                    if r + 1 < R:
-                        transposes(UNITS[r + 1])
                     quantize(UNITS[r])
+                steps = [range(g, g + RUN) for g in range(0, PASSES, RUN)] if r + 1 < R else []
                 room = 512 * CAP if r < R else 512 * 36
                 for x in available(min(r - 1, R - 1), done):
                     u, i, n, lo, hi = x
                     if hi - lo > room:
                         break
                     room -= hi - lo
+                    if steps:
+                        transposes(UNITS[r + 1], steps.pop(0))
                     multiply(x)
                     order.append(x)
                     for k in range(lo // 256, hi // 256):
@@ -242,6 +246,8 @@ def tile_fp8_query_projection_d2_kernel(tc, h, x_bytes, x_scale, w_bytes, w_scal
                     if r >= R and len(order) - closed > 3:
                         finish(order[closed])
                         closed += 1
+                for passes in steps:
+                    transposes(UNITS[r + 1], passes)
                 while r < R and closed < len(order):
                     finish(order[closed])
                     closed += 1

@@ -41,7 +41,8 @@ def tile_fp8_query_projection_d2_kernel(tc, h, x_bytes, x_scale, w_bytes, w_scal
         mpsum = ctx.enter_context(tc.psum_pool(name="mpsum", bufs=4))
 
         ident = const.tile([P, P], F32, name="ident", align_bytes=64)
-        make_identity(nc, ident[:])
+        ones = const.tile([P, P], F32, name="ones", align_bytes=64)
+        ws_row = const.tile([P, (N // B) * (K // B)], F32, name="ws_row", align_bytes=64)
         ws = const.tile([P, (N // B) * (K // B)], F32, name="ws", align_bytes=64)
         xs = const.tile([P, U // P, K // B], F32, name="xs", align_bytes=64)
         bias = const.tile([P, N], BF16, name="bias", align_bytes=64)
@@ -208,18 +209,24 @@ def tile_fp8_query_projection_d2_kernel(tc, h, x_bytes, x_scale, w_bytes, w_scal
 
         with ExitStack() as sched:
             sched.enter_context(tc.manual_schedule())
-            nc.sync.dma_start(out=ws[:], in_=w_scale.rearrange("i j -> (i j)").partition_broadcast(P))
+            nc.vector.memset(ws_row[:], 0.0)
+            nc.gpsimd.memset(ones[:], 1.0)
+            make_identity(nc, ident[:])
+            nc.sync.dma_start(out=ws_row[0:1, :], in_=w_scale.rearrange("(o i) j -> o (i j)", o=1))
             for k, u in enumerate(LOADS):
                 load(u)
-                if k == 1:
-                    nc.sync.dma_start(out=xs[:], in_=x_scale.rearrange("(p i) j -> p i j", p=P))
                 if k == 5:
                     nc.sync.dma_start(out=bias[:], in_=b.partition_broadcast(P))
+                if k == 1:
+                    nc.sync.dma_start(out=xs[:], in_=x_scale.rearrange("(p i) j -> p i j", p=P))
 
             R = len(UNITS)
             done = set()
             order = []
             closed = 0
+            ws_ps = mpsum.tile([P, 512], F32, name="acc")
+            nc.tensor.matmul(ws_ps[:, 0 : (N // B) * (K // B)], lhsT=ones[:], rhs=ws_row[:], start=True, stop=True)
+            nc.vector.tensor_copy(out=ws[:], in_=ws_ps[:, 0 : (N // B) * (K // B)])
             widen(UNITS[0])
             widen(UNITS[1])
             transposes(UNITS[0], range(PASSES))
@@ -232,7 +239,11 @@ def tile_fp8_query_projection_d2_kernel(tc, h, x_bytes, x_scale, w_bytes, w_scal
                     quantize(UNITS[r])
                 steps = [range(g, g + RUN) for g in range(0, PASSES, RUN)] if r + 1 < R else []
                 room = 512 * CAP if r < R else 512 * 36
-                for x in available(min(r - 1, R - 1), done):
+                fresh = available(min(r - 1, R - 1), done)
+                if len(done) + 2 * len(fresh) == 72:
+                    u, i, n, lo, hi = fresh.pop()
+                    fresh += [(u, i, n, 0, 256), (u, i, n, 256, 512)]
+                for x in fresh:
                     u, i, n, lo, hi = x
                     if hi - lo > room:
                         break

from contextlib import ExitStack

import concourse.mybir as mybir
from concourse.masks import make_identity

T, U, K, N, B = 512, 1024, 2048, 1536, 128
FLOPS = 2 * (T + U) * K * N
BYTES = T * K * 2 + U * K + N * K + U * (K // B) * 4 + (N // B) * (K // B) * 4 + N * 2 + (T + U) * N * 4

F32 = mybir.dt.float32
BF16 = mybir.dt.bfloat16
U32 = mybir.dt.uint32
U8 = mybir.dt.uint8
FP8 = mybir.dt.float8_e4m3fn
FP8X4 = mybir.dt.float8_e4m3fn_x4
MULT = mybir.AluOpType.mult
ADD = mybir.AluOpType.add
COPY = mybir.ActivationFunctionType.Copy

P = 128
PASSES = K // 512

UNITS = ["w0a","h0","w0b","h1","w1a","w1b","x0","x1","x2","w2a","w2b","x3"]
LOADS = ["w0a","h0","w0b","h1","w1a","w1b","x0","x1","x2","w2a","w2b","x3"]
SCALAR = ["w0a","w1b","x0","x1","x2","w2a","w2b","x3"]
SHUF = []
RUN = 2
CAP = 3
SHARED = []


def tile_fp8_query_projection_d2_kernel(tc, h, x_bytes, x_scale, w_bytes, w_scale, b, out_0, out_1):
    nc = tc.nc
    with ExitStack() as ctx:
        const = ctx.enter_context(tc.tile_pool(name="const", bufs=1))
        raws = ctx.enter_context(tc.tile_pool(name="raws", bufs=1))
        wides = ctx.enter_context(tc.tile_pool(name="wides", bufs=6))
        groups = ctx.enter_context(tc.tile_pool(name="groups", bufs=3))
        outs = ctx.enter_context(tc.tile_pool(name="outs", bufs=6))
        tpsum = ctx.enter_context(tc.psum_pool(name="tpsum", bufs=1))
        mpsum = ctx.enter_context(tc.psum_pool(name="mpsum", bufs=4))

        ident = const.tile([P, P], F32, name="ident", align_bytes=64)
        ones = const.tile([P, P], F32, name="ones", align_bytes=64)
        ws_row = const.tile([P, (N // B) * (K // B)], F32, name="ws_row", align_bytes=64)
        ws = const.tile([P, (N // B) * (K // B)], F32, name="ws", align_bytes=64)
        xs = const.tile([P, U // P, K // B], F32, name="xs", align_bytes=64)
        bias = const.tile([P, N], BF16, name="bias", align_bytes=64)

        raw = {}
        wide = {}
        bank = {}
        grouped = {}
        codes = {}
        scales = {}
        for n in range(3):
            codes["w%d" % n] = const.tile([P, PASSES, 512], U32, name="wc%d" % n, align_bytes=64)
            scales["w%d" % n] = const.tile([P, PASSES, 512], U8, name="wsc%d" % n, align_bytes=64)
        for u in UNITS:
            if u[0] != "w":
                codes[u] = const.tile([P, PASSES, 256], U32, name="c_" + u, align_bytes=64)
                scales[u] = const.tile([P, PASSES, 256], U8, name="s_" + u, align_bytes=64)

        def row_pair(u):
            if u[0] == "w":
                return 2 * int(u[1]) + (1 if u[2] == "b" else 0)
            return int(u[1])

        def row_tiles(t, u):
            return t.rearrange("(p i) k -> p i k", p=P) if u[0] == "x" else t.rearrange("(i p) k -> p i k", p=P)

        def load(u):
            rp = row_pair(u)
            if u[0] == "h":
                raw[u] = raws.tile([P, 2, K], BF16, name="raw_" + u, align_bytes=64)
                src = h
            else:
                raw[u] = raws.tile([P, 2, K], U8, name="raw_" + u, align_bytes=64)
                src = x_bytes if u[0] == "x" else w_bytes
            cuts = 2 if u == LOADS[0] else 1
            for c in range(cuts):
                cols = slice(c * K // cuts, (c + 1) * K // cuts)
                nc.sync.dma_start(out=raw[u][:, :, cols], in_=row_tiles(src, u)[:, 2 * rp : 2 * rp + 2, cols])

        def contiguous(u, i):
            return (u[0] != "h" and not (u in SCALAR and i == 0)) or u in SHUF

        def widen(u):
            if u[0] == "h":
                if u in SHUF:
                    for i in range(2):
                        wd = wides.tile([P, PASSES, 512], BF16, name="wd%d" % i, align_bytes=64)
                        wide[u, i] = wd
                    for g in range(PASSES):
                        for i in range(2):
                            nc.scalar.copy(
                                out=wide[u, i][:, g, :].bitcast(F32).rearrange("p (u w) -> p u w", u=2),
                                in_=raw[u][:, i, 512 * g : 512 * g + 512].bitcast(F32).rearrange("p (w u) -> p u w", u=2),
                            )
                return
            rp = row_pair(u)
            for i in range(2):
                wd = wides.tile([P, PASSES, 512], BF16, name="wd%d" % i, align_bytes=64)
                wide[u, i] = wd
            for g in range(PASSES):
                for q in range(4):
                    for i in range(2):
                        j = 4 * g + q
                        m = 2 * rp + i
                        sc = ws[:, 16 * m + j : 16 * m + j + 1] if u[0] == "w" else xs[:, m, j : j + 1]
                        src = raw[u][:, i, 128 * j : 128 * j + 128].bitcast(FP8)
                        if u in SCALAR and i == 0:
                            nc.scalar.activation(out=wide[u, i][:, g, 128 * q : 128 * q + 128], in_=src, func=COPY, scale=sc)
                        else:
                            nc.vector.tensor_scalar(
                                out=wide[u, i][:, g, :].rearrange("p (u w e) -> p w u e", u=2, e=2)[:, 32 * q : 32 * q + 32],
                                in0=src.rearrange("p (w u e) -> p w u e", u=2, e=2),
                                scalar1=sc,
                                scalar2=None,
                                op0=MULT,
                            )

        def transposes(u, passes):
            for g in passes:
                bk = tpsum.tile([P, 2, 2, P], F32, name="t%d" % g)
                bank[u, g] = bk
                for i in range(2):
                    if u[0] == "h" and u not in SHUF:
                        words = raw[u][:, i, 512 * g : 512 * g + 512].bitcast(F32)
                    else:
                        words = wide[u, i][:, g, :].bitcast(F32)
                    for t in range(2):
                        src = words[:, P * t : P * t + P] if contiguous(u, i) else words[:, t : 256 : 2]
                        nc.tensor.transpose(bk[:, i, t, :], src, ident[:])

        def evacuate(u):
            gr = groups.tile([P, PASSES, 1024], BF16, name="gr", align_bytes=64)
            grouped[u] = gr
            for g in range(PASSES):
                copy = nc.vector.tensor_copy if u in SHARED and g == PASSES - 1 else nc.scalar.copy
                copy(
                    out=gr[:, g, :].bitcast(F32).rearrange("p (i r u) -> p i r u", i=2, u=2),
                    in_=bank[u, g][:].rearrange("p i u r -> p i r u"),
                )

        def quantize(u):
            gr = grouped[u]
            if u[0] == "w":
                lo = 256 if u[2] == "b" else 0
                key = u[:2]
                for g in range(PASSES):
                    nc.vector.quantize_mx(
                        out=codes[key][:, g, lo : lo + 256].bitcast(FP8X4),
                        scales=scales[key][:, g, lo : lo + 256],
                        in_=gr[:, g, :],
                    )
            else:
                for g in range(0, PASSES, 2):
                    nc.vector.quantize_mx(
                        out=codes[u][:, g : g + 2, :].rearrange("p g c -> p (g c)").bitcast(FP8X4),
                        scales=scales[u][:, g : g + 2, :].rearrange("p g c -> p (g c)"),
                        in_=gr[:, g : g + 2, :].rearrange("p g c -> p (g c)"),
                    )

        acc = {}

        def multiply(grp):
            u, i, n, lo, hi = grp
            ps = mpsum.tile([P, 512], F32, name="acc")
            acc[grp] = ps
            key = "w%d" % n
            for g in range(PASSES):
                nc.tensor.matmul_mx(
                    out=ps[:, 0 : hi - lo],
                    lhsT=codes[u][:, g, P * i : P * i + P].bitcast(FP8X4),
                    lhsT_scale=scales[u][:, g, P * i : P * i + P],
                    rhs=codes[key][:, g, lo:hi].bitcast(FP8X4),
                    rhs_scale=scales[key][:, g, lo:hi],
                    start=(g == 0),
                    stop=(g == PASSES - 1),
                )

        def finish(grp):
            u, i, n, lo, hi = grp
            o = outs.tile([P, 512], F32, name="o", align_bytes=64)
            c0 = 512 * n + lo
            c1 = 512 * n + hi
            nc.vector.tensor_tensor(out=o[:, 0 : hi - lo], in0=acc[grp][:, 0 : hi - lo], in1=bias[:, c0:c1], op=ADD)
            dst = out_0 if u[0] == "h" else out_1
            nc.sync.dma_start(out=row_tiles(dst, u)[:, 2 * row_pair(u) + i, c0:c1], in_=o[:, 0 : hi - lo])

        def available(r, done):
            us = UNITS[: r + 1]
            res = []
            for n in range(3):
                ready = [("w%d%s" % (n, c)) in us for c in "ab"]
                for u in us:
                    if u[0] == "w":
                        continue
                    for i in range(2):
                        left = [ready[k] and (u, i, n, k) not in done for k in range(2)]
                        if left[0] and left[1]:
                            res.append((u, i, n, 0, 512))
                        elif True:
                            for k in range(2):
                                if left[k]:
                                    res.append((u, i, n, 256 * k, 256 * k + 256))
            return res

        with ExitStack() as sched:
            sched.enter_context(tc.manual_schedule())
            nc.vector.memset(ws_row[:], 0.0)
            nc.gpsimd.memset(ones[:], 1.0)
            make_identity(nc, ident[:])
            nc.sync.dma_start(out=ws_row[0:1, :], in_=w_scale.rearrange("(o i) j -> o (i j)", o=1))
            for k, u in enumerate(LOADS):
                load(u)
                if k == 5:
                    nc.sync.dma_start(out=bias[:], in_=b.partition_broadcast(P))
                if k == 1:
                    nc.sync.dma_start(out=xs[:], in_=x_scale.rearrange("(p i) j -> p i j", p=P))

            R = len(UNITS)
            done = set()
            order = []
            closed = 0
            ws_ps = mpsum.tile([P, 512], F32, name="acc")
            nc.tensor.matmul(ws_ps[:, 0 : (N // B) * (K // B)], lhsT=ones[:], rhs=ws_row[:], start=True, stop=True)
            nc.vector.tensor_copy(out=ws[:], in_=ws_ps[:, 0 : (N // B) * (K // B)])
            widen(UNITS[0])
            widen(UNITS[1])
            transposes(UNITS[0], range(PASSES))
            r = 0
            while len(done) < 72:
                if r < R:
                    evacuate(UNITS[r])
                    if r + 2 < R:
                        widen(UNITS[r + 2])
                    quantize(UNITS[r])
                steps = [range(g, g + RUN) for g in range(0, PASSES, RUN)] if r + 1 < R else []
                room = 512 * CAP if r < R else 512 * 36
                fresh = available(min(r - 1, R - 1), done)
                if len(done) + 2 * len(fresh) == 72:
                    u, i, n, lo, hi = fresh.pop()
                    fresh += [(u, i, n, 0, 256), (u, i, n, 256, 512)]
                for x in fresh:
                    u, i, n, lo, hi = x
                    if hi - lo > room:
                        break
                    room -= hi - lo
                    if steps:
                        transposes(UNITS[r + 1], steps.pop(0))
                    multiply(x)
                    order.append(x)
                    for k in range(lo // 256, hi // 256):
                        done.add((u, i, n, k))
                    if r >= R and len(order) - closed > 3:
                        finish(order[closed])
                        closed += 1
                for passes in steps:
                    transposes(UNITS[r + 1], passes)
                while r < R and closed < len(order):
                    finish(order[closed])
                    closed += 1
                r += 1
            while closed < len(order):
                finish(order[closed])
                closed += 1
